import numpy as np
import ml_dtypes


def mxq(x, axis, fmt="e4m3"):
    dtype, down = {"e4m3": (ml_dtypes.float8_e4m3fn, 7), "e5m2": (ml_dtypes.float8_e5m2, 14)}[fmt]
    v = np.moveaxis(np.asarray(x, np.float32).astype(ml_dtypes.bfloat16).astype(np.float64), axis, -1)
    blocks = v.reshape(v.shape[:-1] + (-1, 32))
    amax = np.abs(blocks).max(-1, keepdims=True)
    byte = np.maximum(np.where(amax > 0, np.frexp(amax)[1] - 1 + 127, 0) - down, 1)
    scale = np.exp2(byte - 127.0)
    codes = (blocks / scale).astype(np.float32).astype(dtype).astype(np.float64)
    return np.moveaxis((codes * scale).reshape(v.shape), -1, axis)


WIDE = False


def mx_kscale(k):
    if not WIDE:
        return np.ones(k)
    levels = np.array([10, -10, 5, -5, 0])
    if k % 512:
        return np.exp2(np.random.permutation(np.resize(levels, k // 32))).repeat(32)
    a = np.empty((k // 512, 16))
    for p in range(k // 512):
        a[p, :8] = np.random.permutation(np.resize(levels, 8))
        for g in range(8):
            far = levels[np.abs(levels - a[p, g]) >= 10]
            a[p, g + 8] = far[np.random.randint(len(far))]
    return np.exp2(a.ravel()).repeat(32)


def f64(x):
    return np.asarray(x).astype(np.float64)


def striped(idx):
    return np.tile(np.asarray(idx).reshape(-1, 16).T, (8, 1)).astype(np.uint16)


def unstriped(offs):
    return offs[:16].T.reshape(-1).astype(np.int64)


E2M1 = np.array([0.0, 0.5, 1.0, 1.5, 2.0, 3.0, 4.0, 6.0, -0.0, -0.5, -1.0, -1.5, -2.0, -3.0, -4.0, -6.0])


def pack_weight(w, fmt):
    k, n = w.shape
    w = f64(np.asarray(w, np.float32).astype(ml_dtypes.bfloat16)).reshape(k // 32, 32, n)
    amax = np.abs(w).max(1)
    if fmt == "e4m3":
        byte = np.frexp(amax)[1] - 1 + 127 - 7
    else:
        mant, ex = np.frexp(amax / 6.0)
        byte = np.where(mant > 0.5, ex, ex - 1) + 127
    byte = np.clip(np.where(amax > 0, byte, 1), 1, 254)
    scaled = (w * np.exp2(127.0 - byte)[:, None, :]).reshape(k, n).astype(np.float32)
    by_word = np.ascontiguousarray(scaled.reshape(k // 512, 128, 4, n).transpose(0, 1, 3, 2))
    if fmt == "e4m3":
        words = by_word.astype(ml_dtypes.float8_e4m3fn).view(np.uint8)
    else:
        c = by_word.astype(ml_dtypes.float4_e2m1fn).view(np.uint8) & 0xF
        words = (c[..., 0::2] | (c[..., 1::2] << 4)).reshape(k // 512, 128, 2 * n)
    return np.ascontiguousarray(words), np.ascontiguousarray(byte.astype(np.uint8).reshape(k // 512, 16, n))


def unpack_weight(words, scales, fmt):
    g, _, n = scales.shape
    words = np.ascontiguousarray(words).reshape(g, 128, n, -1)
    if fmt == "e4m3":
        vals = words.view(ml_dtypes.float8_e4m3fn).astype(np.float64)
    else:
        nib = np.empty((g, 128, n, 4), np.uint8)
        nib[..., 0::2] = words & 0xF
        nib[..., 1::2] = words >> 4
        vals = E2M1[nib]
    vals = vals * np.repeat(np.exp2(scales.astype(np.float64) - 127.0), 8, axis=1)[..., None]
    return vals.transpose(0, 1, 3, 2).reshape(g * 512, n)


D, T, G, I, Q, E = 512, 2048, 256, 512, 128, 512


def setup_inputs():
    n = np.random.standard_normal
    idx = np.random.permutation(T)[:G]
    idx2 = np.random.randint(0, G, I)
    idx3 = np.random.randint(0, G, I)
    idx4 = np.random.permutation(T)[:I]
    fd = mx_kscale(D)
    fi = mx_kscale(I)
    ti = np.ones(T)
    ti[idx4] = fi
    keysp = pack_weight(n((D, T)) / fd[:, None], "e4m3")
    return {
        "query": (n((D, Q)) * 0.6 / np.sqrt(D) * fd[:, None]).astype(np.float32),
        "keys_words": keysp[0],
        "keys_scales": keysp[1],
        "near": (np.random.uniform(0.05, 0.95, (1, I))).astype(np.float32),
        "bias": (np.random.uniform(-0.5, 0.5, (1, I))).astype(np.float32),
        "size": (np.random.uniform(0.5, 2.0, (1, I)) * fi).astype(np.float32),
        "vals": (n((E, T)) / ti).astype(np.float32),
        "offs": striped(idx),
        "offs2": striped(idx2),
        "offs3": striped(idx3),
        "offs4": striped(idx4),
    }


def reference(query, keys_words, keys_scales, near, bias, size, vals, offs, offs2, offs3, offs4):
    idx = unstriped(offs)
    idx2 = unstriped(offs2)
    idx3 = unstriped(offs3)
    idx4 = unstriped(offs4)
    keysu = unpack_weight(keys_words, keys_scales, "e4m3")
    queryq = mxq(f64(query), 0, "e4m3")
    keysidxg = keysu[:, idx]
    a = queryq.T @ keysidxg
    s = a[:, idx2] * f64(near) + a[:, idx3] * (1.0 - f64(near)) + f64(bias)
    p = np.exp(s - np.max(s, axis=1, keepdims=True))
    w = p * f64(size) / np.sum(p, axis=1, keepdims=True)
    wt = w.T
    vt = f64(vals)[:, idx4].T
    wtq = mxq(wt, 0, "e4m3")
    vtq = mxq(vt, 0, "e4m3")
    o = wtq.T @ vtq
    return o

@@ -1,0 +1,162 @@
+from contextlib import ExitStack
+
+import concourse.mybir as mybir
+from concourse.masks import make_identity
+
+D, T, G, I, Q, E = 512, 2048, 256, 512, 128, 512
+FLOPS = 2 * D * Q * G + 2 * I * Q * E
+
+F32 = mybir.dt.float32
+BF16 = mybir.dt.bfloat16
+I32 = mybir.dt.int32
+U32 = mybir.dt.uint32
+U16 = mybir.dt.uint16
+U8 = mybir.dt.uint8
+FP8X4 = mybir.dt.float8_e4m3fn_x4
+ALU = mybir.AluOpType
+ACT = mybir.ActivationFunctionType
+AXIS = mybir.AxisListType
+
+P = 128
+PACK = 4
+A_WINDOW = 576
+
+
+def tile_attend_betweenanchors_kernel(tc, query, keys_words, keys_scales, near, bias, size, vals,
+                                       offs, offs2, offs3, offs4, out):
+    nc = tc.nc
+    with ExitStack() as ctx:
+        lists = ctx.enter_context(tc.tile_pool(name="lists", bufs=1))
+        sb = ctx.enter_context(tc.tile_pool(name="sb", bufs=1))
+        ps = ctx.enter_context(tc.psum_pool(name="ps", bufs=1))
+
+        key_bytes = sb.tile([P, T], U8, align_bytes=64)
+        nc.gpsimd.memset(key_bytes[:].bitcast(I32), 0)
+        a_sb = sb.tile([P, A_WINDOW], F32, align_bytes=64)
+        nc.vector.memset(a_sb[:, G:], 0.0)
+        cols = []
+        for name in ("near_col", "bias_col", "size_col"):
+            cols.append(sb.tile([P, PACK], F32, name=name))
+        nc.gpsimd.dma_start(out=cols[0][:], in_=near.rearrange("o (p t) -> (o p) t", t=PACK))
+        ident = sb.tile([P, P], F32, align_bytes=64)
+        make_identity(nc, ident[:])
+        nc.gpsimd.dma_start(out=cols[1][:], in_=bias.rearrange("o (p t) -> (o p) t", t=PACK))
+        nc.gpsimd.dma_start(out=cols[2][:], in_=size.rearrange("o (p t) -> (o p) t", t=PACK))
+
+        q_raw = sb.tile([P, PACK, Q], F32, align_bytes=64)
+        nc.scalar.dma_start(out=q_raw[:], in_=query.rearrange("(p j) q -> p j q", j=PACK))
+        for quad in range(4):
+            nc.scalar.dma_start(out=key_bytes[32 * quad:32 * quad + 4, :].bitcast(I32),
+                                in_=keys_scales[0, 4 * quad:4 * quad + 4, :].bitcast(I32))
+        anchor_list = lists.tile([P, G // 16], U16)
+        nc.sync.dma_start(anchor_list[:], offs)
+        left_list = lists.tile([P, I // 16], U16)
+        nc.sync.dma_start(left_list[:], offs2)
+        right_list = lists.tile([P, I // 16], U16)
+        nc.sync.dma_start(right_list[:], offs3)
+        value_list = lists.tile([P, I // 16], U16)
+        nc.sync.dma_start(value_list[:], offs4)
+        key_words = sb.tile([P, T], I32, align_bytes=64)
+        nc.sync.dma_start(out=key_words[:], in_=keys_words[0].rearrange("p n t -> p (n t)").bitcast(I32))
+        pools = []
+        for c in range(E // P):
+            pool_c = sb.tile([P, T], F32, name="vals%d" % c, align_bytes=64)
+            nc.sync.dma_start(out=pool_c[:], in_=vals[c * P:(c + 1) * P, :])
+            pools.append(pool_c)
+
+        warm = sb.tile([P, 1], F32)
+        nc.scalar.activation(warm[:], ident[:, 0:1], ACT.Exp)
+
+        rows = []
+        for name, col in zip(("near_ps", "bias_ps", "size_ps"), cols):
+            bank = ps.tile([P, PACK, P], F32, name=name)
+            for t in range(PACK):
+                nc.tensor.transpose(bank[:, t, :], col[:, t:t + 1].to_broadcast([P, P]), ident[:])
+            rows.append(bank[:].rearrange("q t p -> q p t"))
+        near_row, bias_row, size_row = rows
+        near_sb = sb.tile([P, I], F32, align_bytes=64)
+        far_sb = sb.tile([P, I], F32, align_bytes=64)
+        nc.scalar.copy(near_sb[:].rearrange("q (p t) -> q p t", t=PACK), near_row)
+        nc.scalar.activation(far_sb[:].rearrange("q (p t) -> q p t", t=PACK), near_row, ACT.Copy,
+                             bias=1.0, scale=-1.0)
+
+        q_bf = sb.tile([P, Q, PACK], BF16, align_bytes=64)
+        nc.vector.tensor_copy(out=q_bf[:], in_=q_raw[:].rearrange("p j q -> p q j"))
+        anchor_bytes = sb.tile([P, G], U8, align_bytes=64)
+        nc.vector.tensor_copy(anchor_bytes[:], key_bytes[:].indirect(anchor_list[:]))
+        q_codes = sb.tile([P, Q], U32, align_bytes=64)
+        q_scales = sb.tile([P, Q], U8, align_bytes=64)
+        nc.vector.quantize_mx(out=q_codes[:].bitcast(FP8X4), scales=q_scales[:],
+                              in_=q_bf[:].rearrange("p q j -> p (q j)"))
+        anchor_words = sb.tile([P, G], U32, align_bytes=64)
+        nc.vector.tensor_copy(anchor_words[:], key_words[:].bitcast(U32).indirect(anchor_list[:]))
+
+        a_ps = ps.tile([P, G], F32, tag="a_w")
+        nc.tensor.matmul_mx(out=a_ps[:], lhsT=q_codes[:].bitcast(FP8X4), lhsT_scale=q_scales[:],
+                            rhs=anchor_words[:].bitcast(FP8X4), rhs_scale=anchor_bytes[:],
+                            start=True, stop=True)
+        nc.scalar.copy(a_sb[:, :G], a_ps[:])
+
+        left = sb.tile([P, I], F32, align_bytes=64)
+        right = sb.tile([P, I], F32, align_bytes=64)
+        nc.vector.tensor_tensor(left[:], a_sb[:].indirect(left_list[:]), near_sb[:], ALU.mult)
+        nc.vector.tensor_tensor(right[:], a_sb[:].indirect(right_list[:]), far_sb[:], ALU.mult)
+        left_b = sb.tile([P, I], F32, align_bytes=64)
+        nc.vector.tensor_tensor(left_b[:].rearrange("q (p t) -> q p t", t=PACK),
+                                left[:].rearrange("q (p t) -> q p t", t=PACK), bias_row, ALU.add)
+        s = sb.tile([P, I], F32, align_bytes=64)
+        nc.vector.tensor_tensor(s[:], left_b[:], right[:], ALU.add)
+        neg_max = sb.tile([P, 1], F32)
+        nc.vector.tensor_reduce(neg_max[:], s[:], AXIS.X, ALU.max, negate=True)
+        p = sb.tile([P, I], F32, align_bytes=64)
+        row_sum = sb.tile([P, 1], F32)
+        nc.scalar.activation(p[:], s[:], ACT.Exp, bias=neg_max[:], scale=1.0, accum_out=row_sum[:])
+        inv_sum = sb.tile([P, 1], F32)
+        nc.vector.reciprocal(inv_sum[:], row_sum[:])
+        w_bf = sb.tile([P, I], BF16, align_bytes=64)
+        nc.vector.scalar_tensor_tensor(w_bf[:].rearrange("q (p t) -> q p t", t=PACK),
+                                       p[:].rearrange("q (p t) -> q p t", t=PACK), inv_sum[:], size_row,
+                                       ALU.mult, ALU.mult)
+
+        picked = []
+        for c in range(E // P):
+            tile_c = sb.tile([P, I], BF16, name="picked%d" % c, align_bytes=64)
+            if c == 0:
+                pool_bf = sb.tile([P, T], BF16, align_bytes=64)
+                nc.scalar.activation(pool_bf[:], pools[c][:], ACT.Copy)
+                nc.scalar.activation(tile_c[:], pool_bf[:].indirect(value_list[:]), ACT.Copy)
+            else:
+                nc.vector.tensor_copy(tile_c[:], pools[c][:].indirect(value_list[:]))
+            picked.append(tile_c)
+
+        def turn_and_quantize(src_bf, name, bank_tag):
+            words = src_bf[:].bitcast(F32)
+            bank = ps.tile([P, 2, P], F32, name=name + "_ps", tag=bank_tag)
+            for u in range(2):
+                nc.tensor.transpose(bank[:, u, :], words[:, u::2], ident[:])
+            grouped = sb.tile([P, P * PACK], BF16, name=name + "_grouped", align_bytes=64)
+            nc.scalar.copy(grouped[:].bitcast(F32).rearrange("p (r u) -> p r u", u=2),
+                           bank[:].rearrange("p u r -> p r u"))
+            codes = sb.tile([P, P], U32, name=name + "_codes", align_bytes=64)
+            scales = sb.tile([P, P], U8, name=name + "_scales", align_bytes=64)
+            nc.vector.quantize_mx(out=codes[:].bitcast(FP8X4), scales=scales[:], in_=grouped[:])
+            return codes, scales
+
+        w_codes, w_scales = turn_and_quantize(w_bf, "w", "a_w")
+        v_ops = []
+        for c in range(E // P):
+            v_ops.append(turn_and_quantize(picked[c], "v%d" % c, "v_bank%d" % (c % 2)))
+
+        for first, count in ((0, 3), (3, 1)):
+            acc = ps.tile([P, count * P], F32, name="acc%d" % first)
+            for c in range(count):
+                codes, scales = v_ops[first + c]
+                nc.tensor.matmul_mx(out=acc[:, c * P:(c + 1) * P], lhsT=w_codes[:].bitcast(FP8X4),
+                                    lhsT_scale=w_scales[:], rhs=codes[:].bitcast(FP8X4),
+                                    rhs_scale=scales[:], start=True, stop=True)
+            result = sb.tile([P, count * P], F32, name="result%d" % first, align_bytes=64)
+            if first == 0:
+                nc.scalar.copy(result[:], acc[:])
+            else:
+                nc.vector.tensor_copy(result[:], acc[:])
+            nc.sync.dma_start(out=out[:, first * P:(first + count) * P], in_=result[:])

@@ -30,65 +30,75 @@ def tile_attend_betweenanchors_kernel(tc, query, keys_words, keys_scales, near, 
         sb = ctx.enter_context(tc.tile_pool(name="sb", bufs=1))
         ps = ctx.enter_context(tc.psum_pool(name="ps", bufs=1))
 
-        key_bytes = sb.tile([P, T], U8, align_bytes=64)
-        nc.gpsimd.memset(key_bytes[:].bitcast(I32), 0)
         a_sb = sb.tile([P, A_WINDOW], F32, align_bytes=64)
         nc.vector.memset(a_sb[:, G:], 0.0)
-        cols = []
-        for name in ("near_col", "bias_col", "size_col"):
-            cols.append(sb.tile([P, PACK], F32, name=name))
-        nc.gpsimd.dma_start(out=cols[0][:], in_=near.rearrange("o (p t) -> (o p) t", t=PACK))
+        key_bytes = sb.tile([P, T], U8, tag="slot3", align_bytes=64)
+        nc.vector.memset(key_bytes[:].bitcast(I32), 0)
         ident = sb.tile([P, P], F32, align_bytes=64)
         make_identity(nc, ident[:])
-        nc.gpsimd.dma_start(out=cols[1][:], in_=bias.rearrange("o (p t) -> (o p) t", t=PACK))
-        nc.gpsimd.dma_start(out=cols[2][:], in_=size.rearrange("o (p t) -> (o p) t", t=PACK))
 
-        q_raw = sb.tile([P, PACK, Q], F32, align_bytes=64)
-        nc.scalar.dma_start(out=q_raw[:], in_=query.rearrange("(p j) q -> p j q", j=PACK))
+        def as_columns(row):
+            return row.rearrange("o (p t) -> (o p) t", t=PACK)
+
+        staged_bytes = sb.tile([P, T], U8, align_bytes=64)
         for quad in range(4):
-            nc.scalar.dma_start(out=key_bytes[32 * quad:32 * quad + 4, :].bitcast(I32),
+            nc.sync.dma_start(out=staged_bytes[32 * quad:32 * quad + 4, :].bitcast(I32),
                                 in_=keys_scales[0, 4 * quad:4 * quad + 4, :].bitcast(I32))
         anchor_list = lists.tile([P, G // 16], U16)
         nc.sync.dma_start(anchor_list[:], offs)
+        q_raw = sb.tile([P, PACK, Q], F32, align_bytes=64)
+        nc.scalar.dma_start(out=q_raw[:], in_=query.rearrange("(p j) q -> p j q", j=PACK))
+        near_col = sb.tile([P, PACK], F32)
+        nc.scalar.dma_start(out=near_col[:], in_=as_columns(near))
+        key_words = sb.tile([P, T], I32, align_bytes=64)
+        nc.sync.dma_start(out=key_words[:], in_=keys_words[0].rearrange("p n t -> p (n t)").bitcast(I32))
         left_list = lists.tile([P, I // 16], U16)
         nc.sync.dma_start(left_list[:], offs2)
         right_list = lists.tile([P, I // 16], U16)
         nc.sync.dma_start(right_list[:], offs3)
+        pools = []
+        for c in range(E // P - 1):
+            pools.append(sb.tile([P, T], F32, name="vals%d" % c, align_bytes=64))
+        nc.sync.dma_start(out=pools[0][:], in_=vals[0:P, :])
         value_list = lists.tile([P, I // 16], U16)
         nc.sync.dma_start(value_list[:], offs4)
-        key_words = sb.tile([P, T], I32, align_bytes=64)
-        nc.sync.dma_start(out=key_words[:], in_=keys_words[0].rearrange("p n t -> p (n t)").bitcast(I32))
-        pools = []
-        for c in range(E // P):
-            pool_c = sb.tile([P, T], F32, name="vals%d" % c, align_bytes=64)
-            nc.sync.dma_start(out=pool_c[:], in_=vals[c * P:(c + 1) * P, :])
-            pools.append(pool_c)
+        bias_col = sb.tile([P, PACK], F32)
+        nc.sync.dma_start(out=bias_col[:], in_=as_columns(bias))
+        size_col = sb.tile([P, PACK], F32)
+        nc.sync.dma_start(out=size_col[:], in_=as_columns(size))
+        for c in range(1, E // P - 1):
+            nc.sync.dma_start(out=pools[c][:], in_=vals[c * P:(c + 1) * P, :])
 
         warm = sb.tile([P, 1], F32)
-        nc.scalar.activation(warm[:], ident[:, 0:1], ACT.Exp)
+        nc.scalar.activation(warm[:], a_sb[:, G:G + 1], ACT.Exp)
+        q_bf = sb.tile([P, Q, PACK], BF16, align_bytes=64)
+        nc.scalar.copy(q_bf[:], q_raw[:].rearrange("p j q -> p q j"))
 
-        rows = []
-        for name, col in zip(("near_ps", "bias_ps", "size_ps"), cols):
-            bank = ps.tile([P, PACK, P], F32, name=name)
+        def spread(col, name, tag):
+            bank = ps.tile([P, PACK, P], F32, name=name, tag=tag)
             for t in range(PACK):
                 nc.tensor.transpose(bank[:, t, :], col[:, t:t + 1].to_broadcast([P, P]), ident[:])
-            rows.append(bank[:].rearrange("q t p -> q p t"))
-        near_row, bias_row, size_row = rows
+            return bank[:].rearrange("q t p -> q p t")
+
+        def by_four(tile):
+            return tile[:].rearrange("q (p t) -> q p t", t=PACK)
+
+        near_row = spread(near_col, "near_ps", "a_w")
         near_sb = sb.tile([P, I], F32, align_bytes=64)
         far_sb = sb.tile([P, I], F32, align_bytes=64)
-        nc.scalar.copy(near_sb[:].rearrange("q (p t) -> q p t", t=PACK), near_row)
-        nc.scalar.activation(far_sb[:].rearrange("q (p t) -> q p t", t=PACK), near_row, ACT.Copy,
-                             bias=1.0, scale=-1.0)
+        nc.scalar.copy(by_four(near_sb), near_row)
+        nc.scalar.activation(by_four(far_sb), near_row, ACT.Copy, bias=1.0, scale=-1.0)
 
-        q_bf = sb.tile([P, Q, PACK], BF16, align_bytes=64)
-        nc.vector.tensor_copy(out=q_bf[:], in_=q_raw[:].rearrange("p j q -> p q j"))
+        for quad in range(4):
+            rows = slice(32 * quad, 32 * quad + 4)
+            nc.vector.tensor_copy(key_bytes[rows, :].bitcast(U16), staged_bytes[rows, :].bitcast(U16))
         anchor_bytes = sb.tile([P, G], U8, align_bytes=64)
         nc.vector.tensor_copy(anchor_bytes[:], key_bytes[:].indirect(anchor_list[:]))
-        q_codes = sb.tile([P, Q], U32, align_bytes=64)
+        q_codes = sb.tile([P, Q], U32, tag="cast", align_bytes=64)
         q_scales = sb.tile([P, Q], U8, align_bytes=64)
         nc.vector.quantize_mx(out=q_codes[:].bitcast(FP8X4), scales=q_scales[:],
                               in_=q_bf[:].rearrange("p q j -> p (q j)"))
-        anchor_words = sb.tile([P, G], U32, align_bytes=64)
+        anchor_words = sb.tile([P, G], U32, tag="slot3", align_bytes=64)
         nc.vector.tensor_copy(anchor_words[:], key_words[:].bitcast(U32).indirect(anchor_list[:]))
 
         a_ps = ps.tile([P, G], F32, tag="a_w")
@@ -97,63 +107,74 @@ def tile_attend_betweenanchors_kernel(tc, query, keys_words, keys_scales, near, 
                             start=True, stop=True)
         nc.scalar.copy(a_sb[:, :G], a_ps[:])
 
+        last_pool = sb.tile([P, T], F32, tag="slot3", align_bytes=64)
+        nc.sync.dma_start(out=last_pool[:], in_=vals[E - P:E, :])
+        pools.append(last_pool)
+        bias_row = spread(bias_col, "bias_ps", "a_w")
+
         left = sb.tile([P, I], F32, align_bytes=64)
         right = sb.tile([P, I], F32, align_bytes=64)
         nc.vector.tensor_tensor(left[:], a_sb[:].indirect(left_list[:]), near_sb[:], ALU.mult)
         nc.vector.tensor_tensor(right[:], a_sb[:].indirect(right_list[:]), far_sb[:], ALU.mult)
-        left_b = sb.tile([P, I], F32, align_bytes=64)
-        nc.vector.tensor_tensor(left_b[:].rearrange("q (p t) -> q p t", t=PACK),
-                                left[:].rearrange("q (p t) -> q p t", t=PACK), bias_row, ALU.add)
+        left_b = sb.tile([P, I], F32, tag="picked1", align_bytes=64)
+        nc.vector.tensor_tensor(by_four(left_b), by_four(left), bias_row, ALU.add)
+        size_row = spread(size_col, "size_ps", "a_w")
         s = sb.tile([P, I], F32, align_bytes=64)
         nc.vector.tensor_tensor(s[:], left_b[:], right[:], ALU.add)
         neg_max = sb.tile([P, 1], F32)
-        nc.vector.tensor_reduce(neg_max[:], s[:], AXIS.X, ALU.max, negate=True)
-        p = sb.tile([P, I], F32, align_bytes=64)
+        neg_s = sb.tile([P, I], F32, align_bytes=64)
+        nc.vector.tensor_scalar(neg_s[:], s[:], -1.0, None, ALU.mult, ALU.min, accum_out=neg_max[:])
+        p = sb.tile([P, I], F32, tag="picked2", align_bytes=64)
         row_sum = sb.tile([P, 1], F32)
-        nc.scalar.activation(p[:], s[:], ACT.Exp, bias=neg_max[:], scale=1.0, accum_out=row_sum[:])
+        nc.scalar.activation(p[:], neg_s[:], ACT.Exp, bias=neg_max[:], scale=-1.0, accum_out=row_sum[:])
         inv_sum = sb.tile([P, 1], F32)
         nc.vector.reciprocal(inv_sum[:], row_sum[:])
-        w_bf = sb.tile([P, I], BF16, align_bytes=64)
-        nc.vector.scalar_tensor_tensor(w_bf[:].rearrange("q (p t) -> q p t", t=PACK),
-                                       p[:].rearrange("q (p t) -> q p t", t=PACK), inv_sum[:], size_row,
-                                       ALU.mult, ALU.mult)
+        w_bf = sb.tile([P, I], BF16, tag="picked3", align_bytes=64)
+        nc.vector.scalar_tensor_tensor(by_four(w_bf), by_four(p), inv_sum[:], size_row, ALU.mult, ALU.mult)
+
+        def turn(src_bf, grouped, name, bank_tag):
+            words = src_bf[:].bitcast(F32)
+            bank = ps.tile([P, 2, P], F32, name=name, tag=bank_tag)
+            for u in range(2):
+                nc.tensor.transpose(bank[:, u, :], words[:, u::2], ident[:])
+            nc.scalar.copy(grouped.bitcast(F32).rearrange("p (r u) -> p r u", u=2),
+                           bank[:].rearrange("p u r -> p r u"))
+
+        w_grouped = sb.tile([P, I], BF16, align_bytes=64)
+        turn(w_bf, w_grouped[:], "w_ps", "a_w")
 
         picked = []
         for c in range(E // P):
-            tile_c = sb.tile([P, I], BF16, name="picked%d" % c, align_bytes=64)
+            tile_c = sb.tile([P, I], BF16, name="picked%d" % c, tag="picked%d" % c, align_bytes=64)
             if c == 0:
-                pool_bf = sb.tile([P, T], BF16, align_bytes=64)
+                pool_bf = sb.tile([P, T], BF16, tag="cast", align_bytes=64)
                 nc.scalar.activation(pool_bf[:], pools[c][:], ACT.Copy)
                 nc.scalar.activation(tile_c[:], pool_bf[:].indirect(value_list[:]), ACT.Copy)
             else:
                 nc.vector.tensor_copy(tile_c[:], pools[c][:].indirect(value_list[:]))
             picked.append(tile_c)
 
-        def turn_and_quantize(src_bf, name, bank_tag):
-            words = src_bf[:].bitcast(F32)
-            bank = ps.tile([P, 2, P], F32, name=name + "_ps", tag=bank_tag)
-            for u in range(2):
-                nc.tensor.transpose(bank[:, u, :], words[:, u::2], ident[:])
-            grouped = sb.tile([P, P * PACK], BF16, name=name + "_grouped", align_bytes=64)
-            nc.scalar.copy(grouped[:].bitcast(F32).rearrange("p (r u) -> p r u", u=2),
-                           bank[:].rearrange("p u r -> p r u"))
-            codes = sb.tile([P, P], U32, name=name + "_codes", align_bytes=64)
-            scales = sb.tile([P, P], U8, name=name + "_scales", align_bytes=64)
-            nc.vector.quantize_mx(out=codes[:].bitcast(FP8X4), scales=scales[:], in_=grouped[:])
-            return codes, scales
+        w_codes = sb.tile([P, Q], U32, align_bytes=64)
+        w_scales = sb.tile([P, Q], U8, align_bytes=64)
+        nc.vector.quantize_mx(out=w_codes[:].bitcast(FP8X4), scales=w_scales[:], in_=w_grouped[:])
 
-        w_codes, w_scales = turn_and_quantize(w_bf, "w", "a_w")
-        v_ops = []
-        for c in range(E // P):
-            v_ops.append(turn_and_quantize(picked[c], "v%d" % c, "v_bank%d" % (c % 2)))
-
-        for first, count in ((0, 3), (3, 1)):
+        for first, runs, tag in ((0, (2, 1), "slot3"), (3, (1,), "last_codes")):
+            count = sum(runs)
+            codes = sb.tile([P, count * P], U32, name="v_codes%d" % first, tag=tag, align_bytes=64)
+            scales = sb.tile([P, count * P], U8, name="v_scales%d" % first, align_bytes=64)
             acc = ps.tile([P, count * P], F32, name="acc%d" % first)
-            for c in range(count):
-                codes, scales = v_ops[first + c]
-                nc.tensor.matmul_mx(out=acc[:, c * P:(c + 1) * P], lhsT=w_codes[:].bitcast(FP8X4),
-                                    lhsT_scale=w_scales[:], rhs=codes[:].bitcast(FP8X4),
-                                    rhs_scale=scales[:], start=True, stop=True)
+            done = 0
+            for run in runs:
+                grouped = sb.tile([P, run * I], BF16, name="v_grouped%d" % (first + done), align_bytes=64)
+                for c in range(run):
+                    block = first + done + c
+                    turn(picked[block], grouped[:, c * I:(c + 1) * I], "v_ps%d" % block, "v_ps%d" % block)
+                cols = slice(done * P, (done + run) * P)
+                nc.vector.quantize_mx(out=codes[:, cols].bitcast(FP8X4), scales=scales[:, cols], in_=grouped[:])
+                nc.tensor.matmul_mx(out=acc[:, cols], lhsT=w_codes[:].bitcast(FP8X4),
+                                    lhsT_scale=w_scales[:], rhs=codes[:, cols].bitcast(FP8X4),
+                                    rhs_scale=scales[:, cols], start=True, stop=True)
+                done = done + run
             result = sb.tile([P, count * P], F32, name="result%d" % first, align_bytes=64)
             if first == 0:
                 nc.scalar.copy(result[:], acc[:])

@@ -15,10 +15,13 @@ U8 = mybir.dt.uint8
 FP8X4 = mybir.dt.float8_e4m3fn_x4
 ALU = mybir.AluOpType
 ACT = mybir.ActivationFunctionType
-AXIS = mybir.AxisListType
 
 P = 128
 PACK = 4
+QUADRANT = 32
+SCALE_ROWS = 4
+LIST_ROWS = 16
+VALUE_BLOCKS = E // P
 A_WINDOW = 576
 
 
@@ -32,7 +35,7 @@ def tile_attend_betweenanchors_kernel(tc, query, keys_words, keys_scales, near, 
 
         a_sb = sb.tile([P, A_WINDOW], F32, align_bytes=64)
         nc.vector.memset(a_sb[:, G:], 0.0)
-        key_bytes = sb.tile([P, T], U8, tag="slot3", align_bytes=64)
+        key_bytes = sb.tile([P, T], U8, tag="keys_then_values", align_bytes=64)
         nc.vector.memset(key_bytes[:].bitcast(I32), 0)
         ident = sb.tile([P, P], F32, align_bytes=64)
         make_identity(nc, ident[:])
@@ -40,42 +43,41 @@ def tile_attend_betweenanchors_kernel(tc, query, keys_words, keys_scales, near, 
         def as_columns(row):
             return row.rearrange("o (p t) -> (o p) t", t=PACK)
 
+        scale_rows = [slice(QUADRANT * quad, QUADRANT * quad + SCALE_ROWS) for quad in range(P // QUADRANT)]
         staged_bytes = sb.tile([P, T], U8, align_bytes=64)
-        for quad in range(4):
-            nc.sync.dma_start(out=staged_bytes[32 * quad:32 * quad + 4, :].bitcast(I32),
-                                in_=keys_scales[0, 4 * quad:4 * quad + 4, :].bitcast(I32))
-        anchor_list = lists.tile([P, G // 16], U16)
+        for quad, rows in enumerate(scale_rows):
+            nc.sync.dma_start(out=staged_bytes[rows, :].bitcast(I32),
+                              in_=keys_scales[0, SCALE_ROWS * quad:SCALE_ROWS * (quad + 1), :].bitcast(I32))
+        anchor_list = lists.tile([P, G // LIST_ROWS], U16)
         nc.sync.dma_start(anchor_list[:], offs)
-        q_raw = sb.tile([P, PACK, Q], F32, align_bytes=64)
-        nc.scalar.dma_start(out=q_raw[:], in_=query.rearrange("(p j) q -> p j q", j=PACK))
         near_col = sb.tile([P, PACK], F32)
         nc.scalar.dma_start(out=near_col[:], in_=as_columns(near))
+        q_raw = sb.tile([P, PACK, Q], F32, align_bytes=64)
+        nc.scalar.dma_start(out=q_raw[:], in_=query.rearrange("(p t) q -> p t q", t=PACK))
         key_words = sb.tile([P, T], I32, align_bytes=64)
         nc.sync.dma_start(out=key_words[:], in_=keys_words[0].rearrange("p n t -> p (n t)").bitcast(I32))
-        left_list = lists.tile([P, I // 16], U16)
+        left_list = lists.tile([P, I // LIST_ROWS], U16)
         nc.sync.dma_start(left_list[:], offs2)
-        right_list = lists.tile([P, I // 16], U16)
+        right_list = lists.tile([P, I // LIST_ROWS], U16)
         nc.sync.dma_start(right_list[:], offs3)
-        pools = []
-        for c in range(E // P - 1):
-            pools.append(sb.tile([P, T], F32, name="vals%d" % c, align_bytes=64))
-        nc.sync.dma_start(out=pools[0][:], in_=vals[0:P, :])
-        value_list = lists.tile([P, I // 16], U16)
+        value_pools = []
+        for block in range(VALUE_BLOCKS - 1):
+            value_pools.append(sb.tile([P, T], F32, name="vals%d" % block, align_bytes=64))
+        nc.sync.dma_start(out=value_pools[0][:], in_=vals[0:P, :])
+        value_list = lists.tile([P, I // LIST_ROWS], U16)
         nc.sync.dma_start(value_list[:], offs4)
         bias_col = sb.tile([P, PACK], F32)
         nc.sync.dma_start(out=bias_col[:], in_=as_columns(bias))
         size_col = sb.tile([P, PACK], F32)
         nc.sync.dma_start(out=size_col[:], in_=as_columns(size))
-        for c in range(1, E // P - 1):
-            nc.sync.dma_start(out=pools[c][:], in_=vals[c * P:(c + 1) * P, :])
+        for block in range(1, VALUE_BLOCKS - 1):
+            nc.sync.dma_start(out=value_pools[block][:], in_=vals[block * P:(block + 1) * P, :])
 
-        warm = sb.tile([P, 1], F32)
-        nc.scalar.activation(warm[:], a_sb[:, G:G + 1], ACT.Exp)
         q_bf = sb.tile([P, Q, PACK], BF16, align_bytes=64)
-        nc.scalar.copy(q_bf[:], q_raw[:].rearrange("p j q -> p q j"))
+        nc.scalar.activation(q_bf[:], q_raw[:].rearrange("p t q -> p q t"), ACT.Copy)
 
-        def spread(col, name, tag):
-            bank = ps.tile([P, PACK, P], F32, name=name, tag=tag)
+        def spread(col, name):
+            bank = ps.tile([P, PACK, P], F32, name=name, tag="chain_bank")
             for t in range(PACK):
                 nc.tensor.transpose(bank[:, t, :], col[:, t:t + 1].to_broadcast([P, P]), ident[:])
             return bank[:].rearrange("q t p -> q p t")
@@ -83,44 +85,43 @@ def tile_attend_betweenanchors_kernel(tc, query, keys_words, keys_scales, near, 
         def by_four(tile):
             return tile[:].rearrange("q (p t) -> q p t", t=PACK)
 
-        near_row = spread(near_col, "near_ps", "a_w")
+        near_row = spread(near_col, "near_ps")
         near_sb = sb.tile([P, I], F32, align_bytes=64)
         far_sb = sb.tile([P, I], F32, align_bytes=64)
-        nc.scalar.copy(by_four(near_sb), near_row)
+        nc.scalar.activation(by_four(near_sb), near_row, ACT.Copy)
         nc.scalar.activation(by_four(far_sb), near_row, ACT.Copy, bias=1.0, scale=-1.0)
 
-        for quad in range(4):
-            rows = slice(32 * quad, 32 * quad + 4)
+        for rows in scale_rows:
             nc.vector.tensor_copy(key_bytes[rows, :].bitcast(U16), staged_bytes[rows, :].bitcast(U16))
         anchor_bytes = sb.tile([P, G], U8, align_bytes=64)
         nc.vector.tensor_copy(anchor_bytes[:], key_bytes[:].indirect(anchor_list[:]))
-        q_codes = sb.tile([P, Q], U32, tag="cast", align_bytes=64)
+        q_codes = sb.tile([P, Q], U32, tag="after_scores", align_bytes=64)
         q_scales = sb.tile([P, Q], U8, align_bytes=64)
         nc.vector.quantize_mx(out=q_codes[:].bitcast(FP8X4), scales=q_scales[:],
-                              in_=q_bf[:].rearrange("p q j -> p (q j)"))
-        anchor_words = sb.tile([P, G], U32, tag="slot3", align_bytes=64)
+                              in_=q_bf[:].rearrange("p q t -> p (q t)"))
+        anchor_words = sb.tile([P, G], U32, tag="keys_then_values", align_bytes=64)
         nc.vector.tensor_copy(anchor_words[:], key_words[:].bitcast(U32).indirect(anchor_list[:]))
 
-        a_ps = ps.tile([P, G], F32, tag="a_w")
+        a_ps = ps.tile([P, G], F32, tag="chain_bank")
         nc.tensor.matmul_mx(out=a_ps[:], lhsT=q_codes[:].bitcast(FP8X4), lhsT_scale=q_scales[:],
                             rhs=anchor_words[:].bitcast(FP8X4), rhs_scale=anchor_bytes[:],
                             start=True, stop=True)
         nc.scalar.copy(a_sb[:, :G], a_ps[:])
 
-        last_pool = sb.tile([P, T], F32, tag="slot3", align_bytes=64)
+        last_pool = sb.tile([P, T], F32, tag="keys_then_values", align_bytes=64)
         nc.sync.dma_start(out=last_pool[:], in_=vals[E - P:E, :])
-        pools.append(last_pool)
-        bias_row = spread(bias_col, "bias_ps", "a_w")
+        value_pools.append(last_pool)
+        bias_row = spread(bias_col, "bias_ps")
 
         left = sb.tile([P, I], F32, align_bytes=64)
         right = sb.tile([P, I], F32, align_bytes=64)
         nc.vector.tensor_tensor(left[:], a_sb[:].indirect(left_list[:]), near_sb[:], ALU.mult)
         nc.vector.tensor_tensor(right[:], a_sb[:].indirect(right_list[:]), far_sb[:], ALU.mult)
-        left_b = sb.tile([P, I], F32, tag="picked1", align_bytes=64)
-        nc.vector.tensor_tensor(by_four(left_b), by_four(left), bias_row, ALU.add)
-        size_row = spread(size_col, "size_ps", "a_w")
+        left_biased = sb.tile([P, I], F32, tag="picked1", align_bytes=64)
+        nc.vector.tensor_tensor(by_four(left_biased), by_four(left), bias_row, ALU.add)
+        size_row = spread(size_col, "size_ps")
         s = sb.tile([P, I], F32, align_bytes=64)
-        nc.vector.tensor_tensor(s[:], left_b[:], right[:], ALU.add)
+        nc.vector.tensor_tensor(s[:], left_biased[:], right[:], ALU.add)
         neg_max = sb.tile([P, 1], F32)
         neg_s = sb.tile([P, I], F32, align_bytes=64)
         nc.vector.tensor_scalar(neg_s[:], s[:], -1.0, None, ALU.mult, ALU.min, accum_out=neg_max[:])
@@ -141,34 +142,34 @@ def tile_attend_betweenanchors_kernel(tc, query, keys_words, keys_scales, near, 
                            bank[:].rearrange("p u r -> p r u"))
 
         w_grouped = sb.tile([P, I], BF16, align_bytes=64)
-        turn(w_bf, w_grouped[:], "w_ps", "a_w")
+        turn(w_bf, w_grouped[:], "w_ps", "chain_bank")
 
         picked = []
-        for c in range(E // P):
-            tile_c = sb.tile([P, I], BF16, name="picked%d" % c, tag="picked%d" % c, align_bytes=64)
-            if c == 0:
-                pool_bf = sb.tile([P, T], BF16, tag="cast", align_bytes=64)
-                nc.scalar.activation(pool_bf[:], pools[c][:], ACT.Copy)
-                nc.scalar.activation(tile_c[:], pool_bf[:].indirect(value_list[:]), ACT.Copy)
+        for block in range(VALUE_BLOCKS):
+            picked_block = sb.tile([P, I], BF16, name="picked%d" % block, tag="picked%d" % block, align_bytes=64)
+            if block == 0:
+                pool_bf = sb.tile([P, T], BF16, tag="after_scores", align_bytes=64)
+                nc.scalar.activation(pool_bf[:], value_pools[block][:], ACT.Copy)
+                nc.scalar.activation(picked_block[:], pool_bf[:].indirect(value_list[:]), ACT.Copy)
             else:
-                nc.vector.tensor_copy(tile_c[:], pools[c][:].indirect(value_list[:]))
-            picked.append(tile_c)
+                nc.vector.tensor_copy(picked_block[:], value_pools[block][:].indirect(value_list[:]))
+            picked.append(picked_block)
 
         w_codes = sb.tile([P, Q], U32, align_bytes=64)
         w_scales = sb.tile([P, Q], U8, align_bytes=64)
         nc.vector.quantize_mx(out=w_codes[:].bitcast(FP8X4), scales=w_scales[:], in_=w_grouped[:])
 
-        for first, runs, tag in ((0, (2, 1), "slot3"), (3, (1,), "last_codes")):
+        for first, runs, codes_tag in ((0, (2, 1), "keys_then_values"), (VALUE_BLOCKS - 1, (1,), "last_codes")):
             count = sum(runs)
-            codes = sb.tile([P, count * P], U32, name="v_codes%d" % first, tag=tag, align_bytes=64)
+            codes = sb.tile([P, count * P], U32, name="v_codes%d" % first, tag=codes_tag, align_bytes=64)
             scales = sb.tile([P, count * P], U8, name="v_scales%d" % first, align_bytes=64)
             acc = ps.tile([P, count * P], F32, name="acc%d" % first)
             done = 0
             for run in runs:
                 grouped = sb.tile([P, run * I], BF16, name="v_grouped%d" % (first + done), align_bytes=64)
-                for c in range(run):
-                    block = first + done + c
-                    turn(picked[block], grouped[:, c * I:(c + 1) * I], "v_ps%d" % block, "v_ps%d" % block)
+                for j in range(run):
+                    block = first + done + j
+                    turn(picked[block], grouped[:, j * I:(j + 1) * I], "v_ps%d" % block, "v_ps%d" % block)
                 cols = slice(done * P, (done + run) * P)
                 nc.vector.quantize_mx(out=codes[:, cols].bitcast(FP8X4), scales=scales[:, cols], in_=grouped[:])
                 nc.tensor.matmul_mx(out=acc[:, cols], lhsT=w_codes[:].bitcast(FP8X4),

from contextlib import ExitStack

import concourse.mybir as mybir
from concourse.masks import make_identity

D, T, G, I, Q, E = 512, 2048, 256, 512, 128, 512
FLOPS = 2 * D * Q * G + 2 * I * Q * E

F32 = mybir.dt.float32
BF16 = mybir.dt.bfloat16
I32 = mybir.dt.int32
U32 = mybir.dt.uint32
U16 = mybir.dt.uint16
U8 = mybir.dt.uint8
FP8X4 = mybir.dt.float8_e4m3fn_x4
ALU = mybir.AluOpType
ACT = mybir.ActivationFunctionType

P = 128
PACK = 4
QUADRANT = 32
SCALE_ROWS = 4
LIST_ROWS = 16
VALUE_BLOCKS = E // P
A_WINDOW = 576


def tile_attend_betweenanchors_kernel(tc, query, keys_words, keys_scales, near, bias, size, vals,
                                       offs, offs2, offs3, offs4, out):
    nc = tc.nc
    with ExitStack() as ctx:
        lists = ctx.enter_context(tc.tile_pool(name="lists", bufs=1))
        sb = ctx.enter_context(tc.tile_pool(name="sb", bufs=1))
        ps = ctx.enter_context(tc.psum_pool(name="ps", bufs=1))

        a_sb = sb.tile([P, A_WINDOW], F32, align_bytes=64)
        nc.vector.memset(a_sb[:, G:], 0.0)
        key_bytes = sb.tile([P, T], U8, tag="keys_then_values", align_bytes=64)
        nc.vector.memset(key_bytes[:].bitcast(I32), 0)
        ident = sb.tile([P, P], F32, align_bytes=64)
        make_identity(nc, ident[:])

        def as_columns(row):
            return row.rearrange("o (p t) -> (o p) t", t=PACK)

        scale_rows = [slice(QUADRANT * quad, QUADRANT * quad + SCALE_ROWS) for quad in range(P // QUADRANT)]
        staged_bytes = sb.tile([P, T], U8, align_bytes=64)
        for quad, rows in enumerate(scale_rows):
            nc.sync.dma_start(out=staged_bytes[rows, :].bitcast(I32),
                              in_=keys_scales[0, SCALE_ROWS * quad:SCALE_ROWS * (quad + 1), :].bitcast(I32))
        anchor_list = lists.tile([P, G // LIST_ROWS], U16)
        nc.sync.dma_start(anchor_list[:], offs)
        near_col = sb.tile([P, PACK], F32)
        nc.scalar.dma_start(out=near_col[:], in_=as_columns(near))
        q_raw = sb.tile([P, PACK, Q], F32, align_bytes=64)
        nc.scalar.dma_start(out=q_raw[:], in_=query.rearrange("(p t) q -> p t q", t=PACK))
        key_words = sb.tile([P, T], I32, align_bytes=64)
        nc.sync.dma_start(out=key_words[:], in_=keys_words[0].rearrange("p n t -> p (n t)").bitcast(I32))
        left_list = lists.tile([P, I // LIST_ROWS], U16)
        nc.sync.dma_start(left_list[:], offs2)
        right_list = lists.tile([P, I // LIST_ROWS], U16)
        nc.sync.dma_start(right_list[:], offs3)
        value_pools = []
        for block in range(VALUE_BLOCKS - 1):
            value_pools.append(sb.tile([P, T], F32, name="vals%d" % block, align_bytes=64))
        nc.sync.dma_start(out=value_pools[0][:], in_=vals[0:P, :])
        value_list = lists.tile([P, I // LIST_ROWS], U16)
        nc.sync.dma_start(value_list[:], offs4)
        bias_col = sb.tile([P, PACK], F32)
        nc.sync.dma_start(out=bias_col[:], in_=as_columns(bias))
        size_col = sb.tile([P, PACK], F32)
        nc.sync.dma_start(out=size_col[:], in_=as_columns(size))
        for block in range(1, VALUE_BLOCKS - 1):
            nc.sync.dma_start(out=value_pools[block][:], in_=vals[block * P:(block + 1) * P, :])

        q_bf = sb.tile([P, Q, PACK], BF16, align_bytes=64)
        nc.scalar.activation(q_bf[:], q_raw[:].rearrange("p t q -> p q t"), ACT.Copy)

        def spread(col, name):
            bank = ps.tile([P, PACK, P], F32, name=name, tag="chain_bank")
            for t in range(PACK):
                nc.tensor.transpose(bank[:, t, :], col[:, t:t + 1].to_broadcast([P, P]), ident[:])
            return bank[:].rearrange("q t p -> q p t")

        def by_four(tile):
            return tile[:].rearrange("q (p t) -> q p t", t=PACK)

        near_row = spread(near_col, "near_ps")
        near_sb = sb.tile([P, I], F32, align_bytes=64)
        far_sb = sb.tile([P, I], F32, align_bytes=64)
        nc.scalar.activation(by_four(near_sb), near_row, ACT.Copy)
        nc.scalar.activation(by_four(far_sb), near_row, ACT.Copy, bias=1.0, scale=-1.0)

        for rows in scale_rows:
            nc.vector.tensor_copy(key_bytes[rows, :].bitcast(U16), staged_bytes[rows, :].bitcast(U16))
        anchor_bytes = sb.tile([P, G], U8, align_bytes=64)
        nc.vector.tensor_copy(anchor_bytes[:], key_bytes[:].indirect(anchor_list[:]))
        q_codes = sb.tile([P, Q], U32, tag="after_scores", align_bytes=64)
        q_scales = sb.tile([P, Q], U8, align_bytes=64)
        nc.vector.quantize_mx(out=q_codes[:].bitcast(FP8X4), scales=q_scales[:],
                              in_=q_bf[:].rearrange("p q t -> p (q t)"))
        anchor_words = sb.tile([P, G], U32, tag="keys_then_values", align_bytes=64)
        nc.vector.tensor_copy(anchor_words[:], key_words[:].bitcast(U32).indirect(anchor_list[:]))

        a_ps = ps.tile([P, G], F32, tag="chain_bank")
        nc.tensor.matmul_mx(out=a_ps[:], lhsT=q_codes[:].bitcast(FP8X4), lhsT_scale=q_scales[:],
                            rhs=anchor_words[:].bitcast(FP8X4), rhs_scale=anchor_bytes[:],
                            start=True, stop=True)
        nc.scalar.copy(a_sb[:, :G], a_ps[:])

        last_pool = sb.tile([P, T], F32, tag="keys_then_values", align_bytes=64)
        nc.sync.dma_start(out=last_pool[:], in_=vals[E - P:E, :])
        value_pools.append(last_pool)
        bias_row = spread(bias_col, "bias_ps")

        left = sb.tile([P, I], F32, align_bytes=64)
        right = sb.tile([P, I], F32, align_bytes=64)
        nc.vector.tensor_tensor(left[:], a_sb[:].indirect(left_list[:]), near_sb[:], ALU.mult)
        nc.vector.tensor_tensor(right[:], a_sb[:].indirect(right_list[:]), far_sb[:], ALU.mult)
        left_biased = sb.tile([P, I], F32, tag="picked1", align_bytes=64)
        nc.vector.tensor_tensor(by_four(left_biased), by_four(left), bias_row, ALU.add)
        size_row = spread(size_col, "size_ps")
        s = sb.tile([P, I], F32, align_bytes=64)
        nc.vector.tensor_tensor(s[:], left_biased[:], right[:], ALU.add)
        neg_max = sb.tile([P, 1], F32)
        neg_s = sb.tile([P, I], F32, align_bytes=64)
        nc.vector.tensor_scalar(neg_s[:], s[:], -1.0, None, ALU.mult, ALU.min, accum_out=neg_max[:])
        p = sb.tile([P, I], F32, tag="picked2", align_bytes=64)
        row_sum = sb.tile([P, 1], F32)
        nc.scalar.activation(p[:], neg_s[:], ACT.Exp, bias=neg_max[:], scale=-1.0, accum_out=row_sum[:])
        inv_sum = sb.tile([P, 1], F32)
        nc.vector.reciprocal(inv_sum[:], row_sum[:])
        w_bf = sb.tile([P, I], BF16, tag="picked3", align_bytes=64)
        nc.vector.scalar_tensor_tensor(by_four(w_bf), by_four(p), inv_sum[:], size_row, ALU.mult, ALU.mult)

        def turn(src_bf, grouped, name, bank_tag):
            words = src_bf[:].bitcast(F32)
            bank = ps.tile([P, 2, P], F32, name=name, tag=bank_tag)
            for u in range(2):
                nc.tensor.transpose(bank[:, u, :], words[:, u::2], ident[:])
            nc.scalar.copy(grouped.bitcast(F32).rearrange("p (r u) -> p r u", u=2),
                           bank[:].rearrange("p u r -> p r u"))

        w_grouped = sb.tile([P, I], BF16, align_bytes=64)
        turn(w_bf, w_grouped[:], "w_ps", "chain_bank")

        picked = []
        for block in range(VALUE_BLOCKS):
            picked_block = sb.tile([P, I], BF16, name="picked%d" % block, tag="picked%d" % block, align_bytes=64)
            if block == 0:
                pool_bf = sb.tile([P, T], BF16, tag="after_scores", align_bytes=64)
                nc.scalar.activation(pool_bf[:], value_pools[block][:], ACT.Copy)
                nc.scalar.activation(picked_block[:], pool_bf[:].indirect(value_list[:]), ACT.Copy)
            else:
                nc.vector.tensor_copy(picked_block[:], value_pools[block][:].indirect(value_list[:]))
            picked.append(picked_block)

        w_codes = sb.tile([P, Q], U32, align_bytes=64)
        w_scales = sb.tile([P, Q], U8, align_bytes=64)
        nc.vector.quantize_mx(out=w_codes[:].bitcast(FP8X4), scales=w_scales[:], in_=w_grouped[:])

        for first, runs, codes_tag in ((0, (2, 1), "keys_then_values"), (VALUE_BLOCKS - 1, (1,), "last_codes")):
            count = sum(runs)
            codes = sb.tile([P, count * P], U32, name="v_codes%d" % first, tag=codes_tag, align_bytes=64)
            scales = sb.tile([P, count * P], U8, name="v_scales%d" % first, align_bytes=64)
            acc = ps.tile([P, count * P], F32, name="acc%d" % first)
            done = 0
            for run in runs:
                grouped = sb.tile([P, run * I], BF16, name="v_grouped%d" % (first + done), align_bytes=64)
                for j in range(run):
                    block = first + done + j
                    turn(picked[block], grouped[:, j * I:(j + 1) * I], "v_ps%d" % block, "v_ps%d" % block)
                cols = slice(done * P, (done + run) * P)
                nc.vector.quantize_mx(out=codes[:, cols].bitcast(FP8X4), scales=scales[:, cols], in_=grouped[:])
                nc.tensor.matmul_mx(out=acc[:, cols], lhsT=w_codes[:].bitcast(FP8X4),
                                    lhsT_scale=w_scales[:], rhs=codes[:, cols].bitcast(FP8X4),
                                    rhs_scale=scales[:, cols], start=True, stop=True)
                done = done + run
            result = sb.tile([P, count * P], F32, name="result%d" % first, align_bytes=64)
            if first == 0:
                nc.scalar.copy(result[:], acc[:])
            else:
                nc.vector.tensor_copy(result[:], acc[:])
            nc.sync.dma_start(out=out[:, first * P:(first + count) * P], in_=result[:])
